import numpy as np
import ml_dtypes


def mxq(x, axis, fmt="e4m3"):
    dtype, down = {"e4m3": (ml_dtypes.float8_e4m3fn, 7), "e5m2": (ml_dtypes.float8_e5m2, 14)}[fmt]
    v = np.moveaxis(np.asarray(x, np.float32).astype(ml_dtypes.bfloat16).astype(np.float64), axis, -1)
    blocks = v.reshape(v.shape[:-1] + (-1, 32))
    amax = np.abs(blocks).max(-1, keepdims=True)
    byte = np.maximum(np.where(amax > 0, np.frexp(amax)[1] - 1 + 127, 0) - down, 1)
    scale = np.exp2(byte - 127.0)
    codes = (blocks / scale).astype(np.float32).astype(dtype).astype(np.float64)
    return np.moveaxis((codes * scale).reshape(v.shape), -1, axis)


WIDE = False


def mx_kscale(k):
    if not WIDE:
        return np.ones(k)
    levels = np.array([10, -10, 5, -5, 0])
    if k % 512:
        return np.exp2(np.random.permutation(np.resize(levels, k // 32))).repeat(32)
    a = np.empty((k // 512, 16))
    for p in range(k // 512):
        a[p, :8] = np.random.permutation(np.resize(levels, 8))
        for g in range(8):
            far = levels[np.abs(levels - a[p, g]) >= 10]
            a[p, g + 8] = far[np.random.randint(len(far))]
    return np.exp2(a.ravel()).repeat(32)


def f64(x):
    return np.asarray(x).astype(np.float64)


E2M1 = np.array([0.0, 0.5, 1.0, 1.5, 2.0, 3.0, 4.0, 6.0, -0.0, -0.5, -1.0, -1.5, -2.0, -3.0, -4.0, -6.0])


def pack_weight(w, fmt):
    k, n = w.shape
    w = f64(np.asarray(w, np.float32).astype(ml_dtypes.bfloat16)).reshape(k // 32, 32, n)
    amax = np.abs(w).max(1)
    if fmt == "e4m3":
        byte = np.frexp(amax)[1] - 1 + 127 - 7
    else:
        mant, ex = np.frexp(amax / 6.0)
        byte = np.where(mant > 0.5, ex, ex - 1) + 127
    byte = np.clip(np.where(amax > 0, byte, 1), 1, 254)
    scaled = (w * np.exp2(127.0 - byte)[:, None, :]).reshape(k, n).astype(np.float32)
    by_word = np.ascontiguousarray(scaled.reshape(k // 512, 128, 4, n).transpose(0, 1, 3, 2))
    if fmt == "e4m3":
        words = by_word.astype(ml_dtypes.float8_e4m3fn).view(np.uint8)
    else:
        c = by_word.astype(ml_dtypes.float4_e2m1fn).view(np.uint8) & 0xF
        words = (c[..., 0::2] | (c[..., 1::2] << 4)).reshape(k // 512, 128, 2 * n)
    return np.ascontiguousarray(words), np.ascontiguousarray(byte.astype(np.uint8).reshape(k // 512, 16, n))


def unpack_weight(words, scales, fmt):
    g, _, n = scales.shape
    words = np.ascontiguousarray(words).reshape(g, 128, n, -1)
    if fmt == "e4m3":
        vals = words.view(ml_dtypes.float8_e4m3fn).astype(np.float64)
    else:
        nib = np.empty((g, 128, n, 4), np.uint8)
        nib[..., 0::2] = words & 0xF
        nib[..., 1::2] = words >> 4
        vals = E2M1[nib]
    vals = vals * np.repeat(np.exp2(scales.astype(np.float64) - 127.0), 8, axis=1)[..., None]
    return vals.transpose(0, 1, 3, 2).reshape(g * 512, n)


def planes(y):
    n, m = y.shape
    v = y.astype(np.float32).astype(ml_dtypes.bfloat16).astype(np.float64).reshape(n // 32, 32, m)
    top = np.abs(v).max(1)
    byte = np.clip(np.where(top > 0, np.frexp(top)[1] - 1 + 127 - 7, 1), 1, 254)
    codes = (v * np.exp2(127.0 - byte)[:, None, :]).reshape(n, m).astype(np.float32).astype(ml_dtypes.float8_e4m3fn).view(np.uint8)
    words = codes.reshape(n // 512, 128, 4, m).transpose(0, 1, 3, 2)
    return np.ascontiguousarray(words), np.ascontiguousarray(byte.astype(np.uint8).reshape(n // 512, 16, m))


D, K, M, T = 128, 512, 1024, 1536


def setup_inputs():
    n = np.random.standard_normal
    s = mx_kscale(K)[:, None]
    p_w0 = pack_weight(n((K, M)) / np.sqrt(K) / s, "e2m1")
    p_w1 = pack_weight(n((K, M)) / np.sqrt(K) / s, "e4m3")
    return {
        "x": (n((K, T + 2 * D)) * s).astype(np.float32),
        "w0_words": p_w0[0],
        "w0_scales": p_w0[1],
        "w1_words": p_w1[0],
        "w1_scales": p_w1[1],
        "w2": (n((K, M)) / np.sqrt(K) / s).astype(np.float32),
    }


def reference(x, w0_words, w0_scales, w1_words, w1_scales, w2):
    x_ = mxq(f64(x), 0, "e4m3")
    w0_ = unpack_weight(w0_words, w0_scales, "e2m1")
    w1_ = unpack_weight(w1_words, w1_scales, "e4m3")
    w2_ = mxq(f64(w2), 0, "e4m3")
    y = w0_.T @ x_[:, :T] + w1_.T @ x_[:, D:D + T] + w2_.T @ x_[:, 2 * D:]
    out_0 = np.maximum(y, 0.0) ** 2
    return (out_0,) + planes(out_0)

@@ -1,0 +1,302 @@
+from contextlib import ExitStack
+
+import concourse.mybir as mybir
+
+D, K, M, T = 128, 512, 1024, 1536
+FLOPS = 2 * 3 * K * M * T
+
+F32 = mybir.dt.float32
+BF16 = mybir.dt.bfloat16
+I32 = mybir.dt.int32
+U32 = mybir.dt.uint32
+U16 = mybir.dt.uint16
+U8 = mybir.dt.uint8
+FP8X4 = mybir.dt.float8_e4m3fn_x4
+FP4X4 = mybir.dt.float4_e2m1fn_x4
+ACT = mybir.ActivationFunctionType
+ALU = mybir.AluOpType
+
+P = 128
+PACK = 4
+HALF = 512
+XW = T + 2 * D
+EARLY = 1024
+
+UNITS = [
+    (0, 0, 512, (1,)),
+    (0, 512, 512, ()),
+    (1, 0, 512, (3,)),
+    (1, 512, 512, (2, 3)),
+    (0, 1024, 512, (2, 3)),
+    (1, 1024, 256, (3,)),
+    (1, 1280, 256, (2, 3)),
+]
+
+
+def tile_mix_dconv_fm_pl_relu2_kernel(
+    tc, x, w0_words, w0_scales, w1_words, w1_scales, w2, out_0, out_1, out_2
+):
+    nc = tc.nc
+    with ExitStack() as ctx:
+        keep = ctx.enter_context(tc.tile_pool(name="keep", bufs=1))
+        ring = ctx.enter_context(tc.tile_pool(name="ring", bufs=3))
+        psum = ctx.enter_context(tc.psum_pool(name="psum", bufs=8))
+        ctx.enter_context(tc.manual_schedule())
+
+        def kept(name, shape, dtype):
+            return keep.tile(shape, dtype, name=name, align_bytes=64)
+
+        x_codes = kept("x_codes", [P, XW], U32)
+        x_scales = kept("x_scales", [P, XW], U8)
+        w0_codes = kept("w0_codes", [P, 2 * M], U8)
+        w0_plane = kept("w0_plane", [P, M], U8)
+        w1_codes = [kept("w1_codes%d" % a, [P, HALF], U32) for a in range(2)]
+        w1_plane = kept("w1_plane", [P, M], U8)
+        w2_codes = [kept("w2_codes%d" % a, [P, HALF], U32) for a in range(2)]
+        w2_plane = [kept("w2_plane%d" % a, [P, HALF], U8) for a in range(2)]
+        w2_bf = [kept("w2_bf%d" % a, [P, PACK * HALF], BF16) for a in range(2)]
+        out_words = [kept("out_words%d" % a, [P, T], U32) for a in range(2)]
+        early_scales = kept("early_scales", [P, 2 * EARLY], U8)
+        late_scales = kept("late_scales", [P, 2 * (T - EARLY)], U8)
+
+        def load_rows(name, src, c0, c1):
+            raw = kept(name, [P, PACK, c1 - c0], F32)
+            nc.sync.dma_start(out=raw[:], in_=src[:, c0:c1].rearrange("(p j) c -> p j c", j=PACK))
+            return raw
+
+        def load_scale_rows(raw, src, rows):
+            for r in rows:
+                nc.sync.dma_start(
+                    out=raw[:].bitcast(I32)[r:P:32, :], in_=src[0].bitcast(I32)[r:16:4, :]
+                )
+
+        def load_w1(a):
+            raw = kept("w1_raw%d" % a, [P, HALF], I32)
+            words = w1_words[0].rearrange("p n i -> p (n i)").bitcast(I32)
+            nc.sync.dma_start(out=raw[:], in_=words[:, a * HALF : (a + 1) * HALF])
+            return raw
+
+        s0_raw = kept("s0_raw", [P, M], U8)
+        s1_raw = kept("s1_raw", [P, M], U8)
+        nc.vector.memset(s0_raw[:].bitcast(I32), 0)
+        nc.vector.memset(s1_raw[:].bitcast(I32), 0)
+
+        w0_raw = kept("w0_raw", [P, 2 * M], U8)
+        nc.sync.dma_start(out=w0_raw[:].bitcast(I32), in_=w0_words[0].bitcast(I32))
+        load_scale_rows(s0_raw, w0_scales, range(4))
+        x_raw0 = load_rows("x_raw0", x, 0, 512)
+        x_raw1 = load_rows("x_raw1", x, 512, 768)
+        w1_raw0 = load_w1(0)
+        load_scale_rows(s1_raw, w1_scales, range(4))
+        w2_raw00 = load_rows("w2_raw00", w2, 0, 256)
+        w2_raw01 = load_rows("w2_raw01", w2, 256, 512)
+        x_raw2 = load_rows("x_raw2", x, 768, 1280)
+        w1_raw1 = load_w1(1)
+        w2_raw1 = load_rows("w2_raw1", w2, 512, 1024)
+        x_raw3 = load_rows("x_raw3", x, 1280, 1792)
+
+        def cast(engine, dst, src):
+            if engine == "scalar":
+                nc.scalar.activation(out=dst, in_=src, func=ACT.Copy)
+            else:
+                nc.vector.tensor_copy(out=dst, in_=src)
+
+        def interleave(engine, dst, src, c0, c1):
+            cast(
+                engine,
+                dst[:, PACK * c0 : PACK * c1].rearrange("p (g e j) -> p g j e", e=4, j=PACK),
+                src[:, :, c0:c1].rearrange("p j (g e) -> p g j e", e=4),
+            )
+
+        def deal_w2(engine, a, raw, m0):
+            count = raw.shape[2] // PACK
+            cast(
+                engine,
+                w2_bf[a][:].rearrange("p (r m j) -> p m j r", r=PACK, j=PACK)[:, m0 : m0 + count],
+                raw[:].rearrange("p j (m r) -> p m j r", r=PACK),
+            )
+
+        def deal_w1(a, raw):
+            nc.vector.tensor_copy(
+                out=w1_codes[a][:].bitcast(I32).rearrange("p (r g e) -> p g r e", r=PACK, e=4),
+                in_=raw[:].rearrange("p (g e r) -> p g r e", r=PACK, e=4),
+            )
+
+        def deal_columns(dst, src):
+            nc.vector.tensor_copy(
+                out=dst.rearrange("p (a r m) -> p a r m", a=2, r=PACK),
+                in_=src.rearrange("p (a m r) -> p a r m", a=2, r=PACK),
+            )
+
+        def quantize(codes, scales, src):
+            nc.vector.quantize_mx(out=codes.bitcast(FP8X4), scales=scales, in_=src)
+
+        def quantize_x(c0, c1, x_bf):
+            quantize(x_codes[:, c0:c1], x_scales[:, c0:c1], x_bf[:])
+
+        def one_pass(acc, tap, a, r, t0, n0, n1, start, stop):
+            cols = slice(r * P, (r + 1) * P)
+            both = slice(a * HALF + r * P, a * HALF + (r + 1) * P)
+            if tap == 0:
+                lhsT = w0_codes[:, 2 * both.start : 2 * both.stop].bitcast(FP4X4)
+                lhsT_scale = w0_plane[:, both]
+            elif tap == 1:
+                lhsT = w1_codes[a][:, cols].bitcast(FP8X4)
+                lhsT_scale = w1_plane[:, both]
+            else:
+                lhsT = w2_codes[a][:, cols].bitcast(FP8X4)
+                lhsT_scale = w2_plane[a][:, cols]
+            window = slice(t0 + tap * D + n0, t0 + tap * D + n1)
+            nc.tensor.matmul_mx(
+                out=acc[:, n0:n1],
+                lhsT=lhsT,
+                lhsT_scale=lhsT_scale,
+                rhs=x_codes[:, window].bitcast(FP8X4),
+                rhs_scale=x_scales[:, window],
+                start=start,
+                stop=stop,
+            )
+
+        def new_banks():
+            banks = []
+            for r in range(PACK):
+                acc = psum.tile([P, 512], F32, name="acc")
+                banks.append(acc)
+            return banks
+
+        def multiply(u):
+            a, t0, width, on_vector = UNITS[u]
+            banks = new_banks()
+            for r in range(PACK):
+                one_pass(banks[r], 1, a, r, t0, 0, width, True, False)
+                step = width if width == 512 else 128
+                for n0 in range(0, width, step):
+                    one_pass(banks[r], 0, a, r, t0, n0, n0 + step, False, False)
+                one_pass(banks[r], 2, a, r, t0, 0, width, False, True)
+            return banks
+
+        def relu_scalar(u, banks, pos):
+            a, t0, width, on_vector = UNITS[u]
+            for r in range(PACK):
+                if r not in on_vector:
+                    nc.scalar.activation(
+                        out=pos[:, r * width : (r + 1) * width], in_=banks[r][:, :width], func=ACT.Relu
+                    )
+
+        def relu_vector(u, banks, pos):
+            a, t0, width, on_vector = UNITS[u]
+            for r in on_vector:
+                nc.vector.tensor_scalar(
+                    out=pos[:, r * width : (r + 1) * width],
+                    in0=banks[r][:, :width],
+                    scalar1=0.0,
+                    scalar2=None,
+                    op0=ALU.max,
+                )
+
+        def square(u, pos):
+            a, t0, width, on_vector = UNITS[u]
+            res = kept("res%d" % u, [P, PACK * width], F32)
+            for h in range(2):
+                cols = slice(2 * h * width, 2 * (h + 1) * width)
+                nc.scalar.activation(out=res[:, cols], in_=pos[:, cols], func=ACT.Square)
+            return res
+
+        def store_result(u, res):
+            a, t0, width, on_vector = UNITS[u]
+            nc.sync.dma_start(
+                out=out_0[a * HALF : (a + 1) * HALF, t0 : t0 + width].rearrange("(p i) t -> p i t", i=PACK),
+                in_=res[:].rearrange("p (i t) -> p i t", i=PACK),
+            )
+
+        def round_result(u, res):
+            a, t0, width, on_vector = UNITS[u]
+            res_bf = ring.tile([P, PACK * width], BF16, name="res_bf", align_bytes=64)
+            interleave("vector", res_bf, res[:].rearrange("p (i t) -> p i t", i=PACK), 0, width)
+            return res_bf
+
+        def quantize_result(u, res_bf):
+            a, t0, width, on_vector = UNITS[u]
+            if t0 < EARLY:
+                scales = early_scales[:, a * EARLY + t0 : a * EARLY + t0 + width]
+            else:
+                first = a * (T - EARLY) + t0 - EARLY
+                scales = late_scales[:, first : first + width]
+            quantize(out_words[a][:, t0 : t0 + width], scales, res_bf[:])
+
+        def store_words(a, t0, t1):
+            nc.sync.dma_start(
+                out=out_1[a].rearrange("p t i -> p (t i)").bitcast(I32)[:, t0:t1],
+                in_=out_words[a][:, t0:t1].bitcast(I32),
+            )
+
+        def store_scales(queues, plane, t0, t1):
+            for q in range(4):
+                queues[q].dma_start(
+                    out=out_2[:, 4 * q : 4 * q + 4, t0:t1].bitcast(I32).rearrange("a r t -> r a t"),
+                    in_=plane[32 * q : 32 * q + 4, :].bitcast(I32).rearrange("r (a t) -> r a t", a=2),
+                )
+
+        deal_columns(w0_codes[:].bitcast(U16), w0_raw[:].bitcast(U16))
+        deal_columns(w0_plane[:], s0_raw[:])
+        x_bf0 = kept("x_bf0", [P, PACK * 512], BF16)
+        interleave("scalar", x_bf0, x_raw0, 0, 176)
+        interleave("vector", x_bf0, x_raw0, 176, 512)
+        x_bf1 = kept("x_bf1", [P, PACK * 256], BF16)
+        interleave("scalar", x_bf1, x_raw1, 0, 256)
+        quantize_x(0, 512, x_bf0)
+        deal_w1(0, w1_raw0)
+        quantize_x(512, 768, x_bf1)
+        deal_columns(w1_plane[:], s1_raw[:])
+        deal_w2("scalar", 0, w2_raw00, 0)
+        deal_w2("vector", 0, w2_raw01, 64)
+        banks = new_banks()
+        for tap in (0, 1):
+            for r in range(PACK):
+                one_pass(banks[r], tap, 0, r, 0, 0, 512, tap == 0, False)
+        for r in range(PACK):
+            cols = slice(r * P, (r + 1) * P)
+            quantize(w2_codes[0][:, cols], w2_plane[0][:, cols], w2_bf[0][:, PACK * r * P : PACK * (r + 1) * P])
+            one_pass(banks[r], 2, 0, r, 0, 0, 512, False, True)
+
+        res = None
+        for u in range(len(UNITS)):
+            width = UNITS[u][2]
+            pos = ring.tile([P, PACK * width], F32, name="pos", align_bytes=64)
+            res_bf = round_result(u - 1, res) if u > 0 else None
+            relu_vector(u, banks, pos)
+            if u == 0:
+                x_bf2 = kept("x_bf2", [P, PACK * 512], BF16)
+                interleave("vector", x_bf2, x_raw2, 0, 512)
+                quantize_x(768, 1280, x_bf2)
+            if u == 1:
+                deal_w2("vector", 1, w2_raw1, 0)
+            if u == 2:
+                x_bf3 = kept("x_bf3", [P, PACK * 512], BF16)
+                interleave("vector", x_bf3, x_raw3, 0, 512)
+            if u > 0:
+                quantize_result(u - 1, res_bf)
+            if u == 1:
+                deal_w1(1, w1_raw1)
+                quantize(w2_codes[1][:], w2_plane[1][:], w2_bf[1][:])
+            if u == 2:
+                quantize_x(1280, 1792, x_bf3)
+            relu_scalar(u, banks, pos)
+            if u + 1 < len(UNITS):
+                banks = multiply(u + 1)
+            res = square(u, pos)
+            if u == 2:
+                store_words(0, 0, EARLY)
+            if u == 4:
+                store_words(1, 0, EARLY)
+                store_scales([nc.sync] * 4, early_scales, 0, EARLY)
+            if u == 5:
+                store_words(0, EARLY, T)
+            if u == 6:
+                store_words(1, 1024, 1280)
+            store_result(u, res)
+        last = len(UNITS) - 1
+        res_bf = round_result(last, res)
+        quantize_result(last, res_bf)
+        store_words(1, 1280, T)
+        store_scales([nc.sync, nc.scalar, nc.sync, nc.scalar], late_scales, EARLY, T)

@@ -23,14 +23,17 @@ XW = T + 2 * D
 EARLY = 1024
 
 UNITS = [
-    (0, 0, 512, (1,)),
-    (0, 512, 512, ()),
-    (1, 0, 512, (3,)),
-    (1, 512, 512, (2, 3)),
-    (0, 1024, 512, (2, 3)),
-    (1, 1024, 256, (3,)),
-    (1, 1280, 256, (2, 3)),
+    (0, 0, 256, ()),
+    (0, 256, 256, ()),
+    (0, 512, 256, ()),
+    (0, 768, 256, ()),
+    (1, 0, 512, (0, 1,)),
+    (1, 512, 512, (0, 1,)),
+    (0, 1024, 512, (0, 1,)),
+    (1, 1024, 256, (0, 1,)),
+    (1, 1280, 256, (0, 1,)),
 ]
+AHEAD = [1, 1, 1, 1, 1, 1, 1, 1, 1, 1]
 
 
 def tile_mix_dconv_fm_pl_relu2_kernel(
@@ -48,7 +51,7 @@ def tile_mix_dconv_fm_pl_relu2_kernel(
 
         x_codes = kept("x_codes", [P, XW], U32)
         x_scales = kept("x_scales", [P, XW], U8)
-        w0_codes = kept("w0_codes", [P, 2 * M], U8)
+        w0_codes = [kept("w0_codes%d" % a, [P, 2 * HALF], U8) for a in range(2)]
         w0_plane = kept("w0_plane", [P, M], U8)
         w1_codes = [kept("w1_codes%d" % a, [P, HALF], U32) for a in range(2)]
         w1_plane = kept("w1_plane", [P, M], U8)
@@ -64,10 +67,10 @@ def tile_mix_dconv_fm_pl_relu2_kernel(
             nc.sync.dma_start(out=raw[:], in_=src[:, c0:c1].rearrange("(p j) c -> p j c", j=PACK))
             return raw
 
-        def load_scale_rows(raw, src, rows):
-            for r in rows:
+        def load_scale_rows(raw, src, first):
+            for r in range(4):
                 nc.sync.dma_start(
-                    out=raw[:].bitcast(I32)[r:P:32, :], in_=src[0].bitcast(I32)[r:16:4, :]
+                    out=raw[:].bitcast(I32)[first + r : P : 32, :], in_=src[0].bitcast(I32)[r:16:4, :]
                 )
 
         def load_w1(a):
@@ -76,24 +79,31 @@ def tile_mix_dconv_fm_pl_relu2_kernel(
             nc.sync.dma_start(out=raw[:], in_=words[:, a * HALF : (a + 1) * HALF])
             return raw
 
+        def load_w0(a):
+            raw = kept("w0_raw%d" % a, [P, 2 * HALF], U8)
+            words = w0_words[0].bitcast(I32)
+            nc.sync.dma_start(out=raw[:].bitcast(I32), in_=words[:, a * 256 : (a + 1) * 256])
+            return raw
+
         s0_raw = kept("s0_raw", [P, M], U8)
         s1_raw = kept("s1_raw", [P, M], U8)
         nc.vector.memset(s0_raw[:].bitcast(I32), 0)
         nc.vector.memset(s1_raw[:].bitcast(I32), 0)
 
-        w0_raw = kept("w0_raw", [P, 2 * M], U8)
-        nc.sync.dma_start(out=w0_raw[:].bitcast(I32), in_=w0_words[0].bitcast(I32))
-        load_scale_rows(s0_raw, w0_scales, range(4))
+        w0_raw0 = load_w0(0)
         x_raw0 = load_rows("x_raw0", x, 0, 512)
-        x_raw1 = load_rows("x_raw1", x, 512, 768)
-        w1_raw0 = load_w1(0)
-        load_scale_rows(s1_raw, w1_scales, range(4))
+        load_scale_rows(s0_raw, w0_scales, 0)
         w2_raw00 = load_rows("w2_raw00", w2, 0, 256)
         w2_raw01 = load_rows("w2_raw01", w2, 256, 512)
-        x_raw2 = load_rows("x_raw2", x, 768, 1280)
+        load_scale_rows(s1_raw, w1_scales, 4)
+        w1_raw0 = load_w1(0)
+        x_raw1 = load_rows("x_raw1", x, 512, 768)
+        x_raw2 = load_rows("x_raw2", x, 768, 1024)
+        x_raw3 = load_rows("x_raw3", x, 1024, 1280)
+        w0_raw1 = load_w0(1)
         w1_raw1 = load_w1(1)
         w2_raw1 = load_rows("w2_raw1", w2, 512, 1024)
-        x_raw3 = load_rows("x_raw3", x, 1280, 1792)
+        x_raw4 = load_rows("x_raw4", x, 1280, 1792)
 
         def cast(engine, dst, src):
             if engine == "scalar":
@@ -108,12 +118,11 @@ def tile_mix_dconv_fm_pl_relu2_kernel(
                 src[:, :, c0:c1].rearrange("p j (g e) -> p g j e", e=4),
             )
 
-        def deal_w2(engine, a, raw, m0):
-            count = raw.shape[2] // PACK
+        def deal_w2(engine, a, raw, m0, lo, hi):
             cast(
                 engine,
-                w2_bf[a][:].rearrange("p (r m j) -> p m j r", r=PACK, j=PACK)[:, m0 : m0 + count],
-                raw[:].rearrange("p j (m r) -> p m j r", r=PACK),
+                w2_bf[a][:].rearrange("p (r m j) -> p m j r", r=PACK, j=PACK)[:, m0 + lo : m0 + hi],
+                raw[:].rearrange("p j (m r) -> p m j r", r=PACK)[:, lo:hi],
             )
 
         def deal_w1(a, raw):
@@ -122,27 +131,40 @@ def tile_mix_dconv_fm_pl_relu2_kernel(
                 in_=raw[:].rearrange("p (g e r) -> p g r e", r=PACK, e=4),
             )
 
+        def deal_w0(a, raw):
+            nc.vector.tensor_copy(
+                out=w0_codes[a][:].bitcast(U16).rearrange("p (h r m) -> p h r m", h=2, r=2),
+                in_=raw[:].bitcast(U16).rearrange("p (m h r) -> p h r m", h=2, r=2),
+            )
+
         def deal_columns(dst, src):
             nc.vector.tensor_copy(
                 out=dst.rearrange("p (a r m) -> p a r m", a=2, r=PACK),
                 in_=src.rearrange("p (a m r) -> p a r m", a=2, r=PACK),
             )
 
+        def deal_scales(dst, src, a):
+            cols = slice(a * HALF, (a + 1) * HALF)
+            nc.vector.tensor_copy(
+                out=dst[:, cols].rearrange("p (h r m) -> p h r m", h=2, r=2),
+                in_=src[:, cols].rearrange("p (m h r) -> p h r m", h=2, r=2),
+            )
+
         def quantize(codes, scales, src):
             nc.vector.quantize_mx(out=codes.bitcast(FP8X4), scales=scales, in_=src)
 
         def quantize_x(c0, c1, x_bf):
-            quantize(x_codes[:, c0:c1], x_scales[:, c0:c1], x_bf[:])
+            quantize(x_codes[:, c0:c1], x_scales[:, c0:c1], x_bf)
 
         def one_pass(acc, tap, a, r, t0, n0, n1, start, stop):
             cols = slice(r * P, (r + 1) * P)
             both = slice(a * HALF + r * P, a * HALF + (r + 1) * P)
             if tap == 0:
-                lhsT = w0_codes[:, 2 * both.start : 2 * both.stop].bitcast(FP4X4)
+                lhsT = w0_codes[a][:, 2 * cols.start : 2 * cols.stop].bitcast(FP4X4)
                 lhsT_scale = w0_plane[:, both]
             elif tap == 1:
                 lhsT = w1_codes[a][:, cols].bitcast(FP8X4)
-                lhsT_scale = w1_plane[:, both]
+                lhsT_scale = w1_plane[4:, both]
             else:
                 lhsT = w2_codes[a][:, cols].bitcast(FP8X4)
                 lhsT_scale = w2_plane[a][:, cols]
@@ -164,49 +186,46 @@ def tile_mix_dconv_fm_pl_relu2_kernel(
                 banks.append(acc)
             return banks
 
-        def multiply(u):
+        def multiply(u, banks, rows, taps):
             a, t0, width, on_vector = UNITS[u]
-            banks = new_banks()
-            for r in range(PACK):
-                one_pass(banks[r], 1, a, r, t0, 0, width, True, False)
-                step = width if width == 512 else 128
-                for n0 in range(0, width, step):
-                    one_pass(banks[r], 0, a, r, t0, n0, n0 + step, False, False)
-                one_pass(banks[r], 2, a, r, t0, 0, width, False, True)
-            return banks
+            for r in rows:
+                for tap in taps:
+                    step = 128 if tap == 0 and width < 512 else width
+                    for n0 in range(0, width, step):
+                        one_pass(banks[r], tap, a, r, t0, n0, n0 + step, tap == 0 and n0 == 0, tap == 2)
 
-        def relu_scalar(u, banks, pos):
-            a, t0, width, on_vector = UNITS[u]
-            for r in range(PACK):
-                if r not in on_vector:
-                    nc.scalar.activation(
-                        out=pos[:, r * width : (r + 1) * width], in_=banks[r][:, :width], func=ACT.Relu
-                    )
+        def relu_scalar(u, r):
+            width = UNITS[u][2]
+            nc.scalar.activation(
+                out=pos[u][:, r * width : (r + 1) * width], in_=banks[u][r][:, :width], func=ACT.Relu
+            )
 
-        def relu_vector(u, banks, pos):
-            a, t0, width, on_vector = UNITS[u]
-            for r in on_vector:
-                nc.vector.tensor_scalar(
-                    out=pos[:, r * width : (r + 1) * width],
-                    in0=banks[r][:, :width],
-                    scalar1=0.0,
-                    scalar2=None,
-                    op0=ALU.max,
-                )
+        def relu_vector(u, r):
+            width = UNITS[u][2]
+            nc.vector.tensor_scalar(
+                out=pos[u][:, r * width : (r + 1) * width],
+                in0=banks[u][r][:, :width],
+                scalar1=0.0,
+                scalar2=None,
+                op0=ALU.max,
+            )
 
-        def square(u, pos):
-            a, t0, width, on_vector = UNITS[u]
-            res = kept("res%d" % u, [P, PACK * width], F32)
-            for h in range(2):
-                cols = slice(2 * h * width, 2 * (h + 1) * width)
-                nc.scalar.activation(out=res[:, cols], in_=pos[:, cols], func=ACT.Square)
-            return res
+        def square(u, r0, r1):
+            width = UNITS[u][2]
+            cols = slice(r0 * width, r1 * width)
+            nc.scalar.activation(out=res[u][:, cols], in_=pos[u][:, cols], func=ACT.Square)
 
-        def store_result(u, res):
+        def square_vector(u, r0, r1):
+            width = UNITS[u][2]
+            cols = slice(r0 * width, r1 * width)
+            nc.vector.tensor_tensor(out=res[u][:, cols], in0=pos[u][:, cols], in1=pos[u][:, cols], op=ALU.mult)
+
+        def store_result(u, res, i0, i1):
             a, t0, width, on_vector = UNITS[u]
+            rows = out_0[a * HALF : (a + 1) * HALF, t0 : t0 + width].rearrange("(p i) t -> p i t", i=PACK)
             nc.sync.dma_start(
-                out=out_0[a * HALF : (a + 1) * HALF, t0 : t0 + width].rearrange("(p i) t -> p i t", i=PACK),
-                in_=res[:].rearrange("p (i t) -> p i t", i=PACK),
+                out=rows[:, i0:i1, :],
+                in_=res[:, i0 * width : i1 * width].rearrange("p (i t) -> p i t", t=width),
             )
 
         def round_result(u, res):
@@ -237,66 +256,98 @@ def tile_mix_dconv_fm_pl_relu2_kernel(
                     in_=plane[32 * q : 32 * q + 4, :].bitcast(I32).rearrange("r (a t) -> r a t", a=2),
                 )
 
-        deal_columns(w0_codes[:].bitcast(U16), w0_raw[:].bitcast(U16))
-        deal_columns(w0_plane[:], s0_raw[:])
+        def open_unit(u):
+            banks.append(new_banks())
+            tile = ring.tile([P, PACK * UNITS[u][2]], F32, name="pos", align_bytes=64)
+            pos.append(tile)
+            res.append(kept("res%d" % u, [P, PACK * UNITS[u][2]], F32))
+
+        rows = range(PACK)
+        banks, pos, res = [], [], []
         x_bf0 = kept("x_bf0", [P, PACK * 512], BF16)
-        interleave("scalar", x_bf0, x_raw0, 0, 176)
-        interleave("vector", x_bf0, x_raw0, 176, 512)
         x_bf1 = kept("x_bf1", [P, PACK * 256], BF16)
-        interleave("scalar", x_bf1, x_raw1, 0, 256)
-        quantize_x(0, 512, x_bf0)
-        deal_w1(0, w1_raw0)
-        quantize_x(512, 768, x_bf1)
-        deal_columns(w1_plane[:], s1_raw[:])
-        deal_w2("scalar", 0, w2_raw00, 0)
-        deal_w2("vector", 0, w2_raw01, 64)
-        banks = new_banks()
-        for tap in (0, 1):
-            for r in range(PACK):
-                one_pass(banks[r], tap, 0, r, 0, 0, 512, tap == 0, False)
-        for r in range(PACK):
+        x_bf2 = kept("x_bf2", [P, PACK * 256], BF16)
+        x_bf3 = kept("x_bf3", [P, PACK * 256], BF16)
+        x_bf4 = kept("x_bf4", [P, PACK * 512], BF16)
+        deal_w0(0, w0_raw0)
+        interleave("vector", x_bf0, x_raw0, 0, 256)
+        interleave("scalar", x_bf0, x_raw0, 256, 512)
+        deal_columns(w0_plane[:], s0_raw[:])
+        quantize_x(0, 256, x_bf0[:, :1024])
+        deal_w2("scalar", 0, w2_raw00, 0, 0, 64)
+        quantize_x(256, 512, x_bf0[:, 1024:])
+        deal_w2("vector", 0, w2_raw01, 64, 0, 44)
+        deal_w2("scalar", 0, w2_raw01, 64, 44, 64)
+        deal_scales(w1_plane, s1_raw, 0)
+        open_unit(0)
+        open_unit(1)
+        multiply(0, banks[0], rows, (0,))
+        multiply(1, banks[1], rows, (0,))
+        for r in rows:
             cols = slice(r * P, (r + 1) * P)
             quantize(w2_codes[0][:, cols], w2_plane[0][:, cols], w2_bf[0][:, PACK * r * P : PACK * (r + 1) * P])
-            one_pass(banks[r], 2, 0, r, 0, 0, 512, False, True)
+            if r == 0:
+                deal_w1(0, w1_raw0)
+            multiply(0, banks[0], (r,), (1, 2))
+        interleave("scalar", x_bf1, x_raw1, 0, 96)
+        interleave("vector", x_bf1, x_raw1, 96, 256)
+        quantize_x(512, 768, x_bf1[:])
+        multiply(1, banks[1], rows, (1, 2))
 
-        res = None
+        last = len(UNITS) - 1
+        res_bf = None
         for u in range(len(UNITS)):
-            width = UNITS[u][2]
-            pos = ring.tile([P, PACK * width], F32, name="pos", align_bytes=64)
-            res_bf = round_result(u - 1, res) if u > 0 else None
-            relu_vector(u, banks, pos)
+            a, t0, width, on_vector = UNITS[u]
+            on_scalar = [r for r in rows if r not in on_vector]
+            ahead = ()
+            if 0 < u < last:
+                open_unit(u + 1)
+                multiply(u + 1, banks[u + 1], rows, (0, 1, 2))
+                ahead = UNITS[u + 1][3]
             if u == 0:
-                x_bf2 = kept("x_bf2", [P, PACK * 512], BF16)
-                interleave("vector", x_bf2, x_raw2, 0, 512)
-                quantize_x(768, 1280, x_bf2)
+                interleave("vector", x_bf2, x_raw2, 0, 256)
             if u == 1:
-                deal_w2("vector", 1, w2_raw1, 0)
+                interleave("vector", x_bf3, x_raw3, 0, 256)
             if u == 2:
-                x_bf3 = kept("x_bf3", [P, PACK * 512], BF16)
-                interleave("vector", x_bf3, x_raw3, 0, 512)
+                deal_w2("vector", 1, w2_raw1, 0, 0, 128)
+            if u == 3:
+                interleave("vector", x_bf4, x_raw4, 0, 512)
+            if u > 0:
+                res_bf = round_result(u - 1, res[u - 1])
+            for r in ahead[:AHEAD[u + 1]]:
+                relu_vector(u + 1, r)
+            if u == 0:
+                quantize_x(768, 1024, x_bf2[:])
+            if u == 1:
+                quantize_x(1024, 1280, x_bf3[:])
+            if u == 2:
+                quantize(w2_codes[1][:], w2_plane[1][:], w2_bf[1][:])
+            if u == 3:
+                quantize_x(1280, 1792, x_bf4[:])
             if u > 0:
                 quantize_result(u - 1, res_bf)
             if u == 1:
+                deal_w0(1, w0_raw1)
                 deal_w1(1, w1_raw1)
-                quantize(w2_codes[1][:], w2_plane[1][:], w2_bf[1][:])
-            if u == 2:
-                quantize_x(1280, 1792, x_bf3)
-            relu_scalar(u, banks, pos)
-            if u + 1 < len(UNITS):
-                banks = multiply(u + 1)
-            res = square(u, pos)
-            if u == 2:
-                store_words(0, 0, EARLY)
-            if u == 4:
-                store_words(1, 0, EARLY)
-                store_scales([nc.sync] * 4, early_scales, 0, EARLY)
-            if u == 5:
-                store_words(0, EARLY, T)
+                deal_scales(w1_plane, s1_raw, 1)
+            relu_scalar(u, on_scalar[0])
+            for n in range(len(on_scalar)):
+                if n + 1 < len(on_scalar):
+                    relu_scalar(u, on_scalar[n + 1])
+                square(u, on_scalar[n], on_scalar[n] + 1)
+            for r in ahead[AHEAD[u + 1]:]:
+                relu_vector(u + 1, r)
+            split = len(on_vector)
+            store_result(u, res[u], split, 4)
+            if u > 0:
+                before = UNITS[u - 1]
+                store_words(before[0], before[1], before[1] + before[2])
+            if split > 0:
+                square(u, 0, split)
+                store_result(u, res[u], 0, split)
             if u == 6:
-                store_words(1, 1024, 1280)
-            store_result(u, res)
-        last = len(UNITS) - 1
-        res_bf = round_result(last, res)
+                store_scales([nc.sync] * 4, early_scales, 0, EARLY)
+        res_bf = round_result(last, res[last])
         quantize_result(last, res_bf)
-        store_words(1, 1280, T)
+        store_words(1, UNITS[last][1], T)
         store_scales([nc.sync, nc.scalar, nc.sync, nc.scalar], late_scales, EARLY, T)

@@ -18,28 +18,32 @@ ALU = mybir.AluOpType
 
 P = 128
 PACK = 4
-HALF = 512
-XW = T + 2 * D
-EARLY = 1024
+HALF = P * PACK
+BANK = 512
+NARROW = BANK // 2
+FP4_NARROW = 128
+LINE = 4
+W1_PLANE = 4
+EARLY = 2 * BANK
 
-UNITS = [
-    (0, 0, 256, ()),
-    (0, 256, 256, ()),
-    (0, 512, 256, ()),
-    (0, 768, 256, ()),
-    (1, 0, 512, (0, 1,)),
-    (1, 512, 512, (0, 1,)),
-    (0, 1024, 512, (0, 1,)),
-    (1, 1024, 256, (0, 1,)),
-    (1, 1280, 256, (0, 1,)),
-]
-AHEAD = [1, 1, 1, 1, 1, 1, 1, 1, 1, 1]
+TILES = [(0, 0), (0, BANK), (1, 0), (1, BANK), (0, 2 * BANK), (1, 2 * BANK)]
+NARROW_TILES = (0, 1, len(TILES) - 1)
+X_CUTS = [0, 512, 768, 1024, 1280, T + 2 * D]
+W2_ON_VECTOR = 84
+LAST_ON_SCALAR = 72
 
 
 def tile_mix_dconv_fm_pl_relu2_kernel(
     tc, x, w0_words, w0_scales, w1_words, w1_scales, w2, out_0, out_1, out_2
 ):
     nc = tc.nc
+    steps = []
+    for tile in range(len(TILES)):
+        width = NARROW if tile in NARROW_TILES else BANK
+        steps.extend((tile, c0, width) for c0 in range(0, BANK, width))
+    last = len(steps) - 1
+    first_wide = 4
+
     with ExitStack() as ctx:
         keep = ctx.enter_context(tc.tile_pool(name="keep", bufs=1))
         ring = ctx.enter_context(tc.tile_pool(name="ring", bufs=3))
@@ -49,8 +53,8 @@ def tile_mix_dconv_fm_pl_relu2_kernel(
         def kept(name, shape, dtype):
             return keep.tile(shape, dtype, name=name, align_bytes=64)
 
-        x_codes = kept("x_codes", [P, XW], U32)
-        x_scales = kept("x_scales", [P, XW], U8)
+        x_codes = kept("x_codes", [P, X_CUTS[-1]], U32)
+        x_plane = kept("x_plane", [P, X_CUTS[-1]], U8)
         w0_codes = [kept("w0_codes%d" % a, [P, 2 * HALF], U8) for a in range(2)]
         w0_plane = kept("w0_plane", [P, M], U8)
         w1_codes = [kept("w1_codes%d" % a, [P, HALF], U32) for a in range(2)]
@@ -58,13 +62,32 @@ def tile_mix_dconv_fm_pl_relu2_kernel(
         w2_codes = [kept("w2_codes%d" % a, [P, HALF], U32) for a in range(2)]
         w2_plane = [kept("w2_plane%d" % a, [P, HALF], U8) for a in range(2)]
         w2_bf = [kept("w2_bf%d" % a, [P, PACK * HALF], BF16) for a in range(2)]
-        out_words = [kept("out_words%d" % a, [P, T], U32) for a in range(2)]
-        early_scales = kept("early_scales", [P, 2 * EARLY], U8)
-        late_scales = kept("late_scales", [P, 2 * (T - EARLY)], U8)
+        x_bf = [
+            kept("x_bf%d" % n, [P, PACK * (X_CUTS[n + 1] - X_CUTS[n])], BF16) for n in range(len(X_CUTS) - 1)
+        ]
+        res = [kept("res%d" % tile, [P, PACK, BANK], F32) for tile in range(len(TILES))]
+        out_codes = [kept("out_codes%d" % a, [P, T], U32) for a in range(2)]
+        early_plane = kept("early_plane", [P, 2 * EARLY], U8)
+        late_plane = kept("late_plane", [P, 2 * (T - EARLY)], U8)
 
         def load_rows(name, src, c0, c1):
             raw = kept(name, [P, PACK, c1 - c0], F32)
             nc.sync.dma_start(out=raw[:], in_=src[:, c0:c1].rearrange("(p j) c -> p j c", j=PACK))
+            return raw
+
+        def load_x(n):
+            return load_rows("x_raw%d" % n, x, X_CUTS[n], X_CUTS[n + 1])
+
+        def load_w0(a):
+            raw = kept("w0_raw%d" % a, [P, 2 * HALF], U8)
+            pairs = w0_words[0].bitcast(I32)
+            nc.sync.dma_start(out=raw[:].bitcast(I32), in_=pairs[:, a * HALF // 2 : (a + 1) * HALF // 2])
+            return raw
+
+        def load_w1(a):
+            raw = kept("w1_raw%d" % a, [P, HALF], I32)
+            words = w1_words[0].rearrange("p n i -> p (n i)").bitcast(I32)
+            nc.sync.dma_start(out=raw[:], in_=words[:, a * HALF : (a + 1) * HALF])
             return raw
 
         def load_scale_rows(raw, src, first):
@@ -73,281 +96,267 @@ def tile_mix_dconv_fm_pl_relu2_kernel(
                     out=raw[:].bitcast(I32)[first + r : P : 32, :], in_=src[0].bitcast(I32)[r:16:4, :]
                 )
 
-        def load_w1(a):
-            raw = kept("w1_raw%d" % a, [P, HALF], I32)
-            words = w1_words[0].rearrange("p n i -> p (n i)").bitcast(I32)
-            nc.sync.dma_start(out=raw[:], in_=words[:, a * HALF : (a + 1) * HALF])
-            return raw
-
-        def load_w0(a):
-            raw = kept("w0_raw%d" % a, [P, 2 * HALF], U8)
-            words = w0_words[0].bitcast(I32)
-            nc.sync.dma_start(out=raw[:].bitcast(I32), in_=words[:, a * 256 : (a + 1) * 256])
-            return raw
-
         s0_raw = kept("s0_raw", [P, M], U8)
         s1_raw = kept("s1_raw", [P, M], U8)
         nc.vector.memset(s0_raw[:].bitcast(I32), 0)
         nc.vector.memset(s1_raw[:].bitcast(I32), 0)
 
-        w0_raw0 = load_w0(0)
-        x_raw0 = load_rows("x_raw0", x, 0, 512)
+        w0_raw, w1_raw, w2_raw, x_raw = [], [], [], []
+        w0_raw.append(load_w0(0))
+        x_raw.append(load_x(0))
         load_scale_rows(s0_raw, w0_scales, 0)
-        w2_raw00 = load_rows("w2_raw00", w2, 0, 256)
-        w2_raw01 = load_rows("w2_raw01", w2, 256, 512)
-        load_scale_rows(s1_raw, w1_scales, 4)
-        w1_raw0 = load_w1(0)
-        x_raw1 = load_rows("x_raw1", x, 512, 768)
-        x_raw2 = load_rows("x_raw2", x, 768, 1024)
-        x_raw3 = load_rows("x_raw3", x, 1024, 1280)
-        w0_raw1 = load_w0(1)
-        w1_raw1 = load_w1(1)
-        w2_raw1 = load_rows("w2_raw1", w2, 512, 1024)
-        x_raw4 = load_rows("x_raw4", x, 1280, 1792)
+        w2_raw.append(load_rows("w2_raw0", w2, 0, HALF))
+        load_scale_rows(s1_raw, w1_scales, W1_PLANE)
+        w1_raw.append(load_w1(0))
+        x_raw.extend(load_x(n) for n in (1, 2, 3))
+        w0_raw.append(load_w0(1))
+        w1_raw.append(load_w1(1))
+        w2_raw.append(load_rows("w2_raw1", w2, HALF, M))
+        x_raw.append(load_x(4))
 
-        def cast(engine, dst, src):
-            if engine == "scalar":
-                nc.scalar.activation(out=dst, in_=src, func=ACT.Copy)
-            else:
-                nc.vector.tensor_copy(out=dst, in_=src)
+        def round_on_vector(dst, src):
+            nc.vector.tensor_copy(out=dst, in_=src)
 
-        def interleave(engine, dst, src, c0, c1):
-            cast(
-                engine,
-                dst[:, PACK * c0 : PACK * c1].rearrange("p (g e j) -> p g j e", e=4, j=PACK),
-                src[:, :, c0:c1].rearrange("p j (g e) -> p g j e", e=4),
+        def round_on_scalar(dst, src):
+            nc.scalar.activation(out=dst, in_=src, func=ACT.Copy)
+
+        def interleave(rounder, dst, src, c0, c1):
+            rounder(
+                dst[:, PACK * c0 : PACK * c1].rearrange("p (g e j) -> p g j e", e=LINE, j=PACK),
+                src[:, :, c0:c1].rearrange("p j (g e) -> p g j e", e=LINE),
             )
 
-        def deal_w2(engine, a, raw, m0, lo, hi):
-            cast(
-                engine,
-                w2_bf[a][:].rearrange("p (r m j) -> p m j r", r=PACK, j=PACK)[:, m0 + lo : m0 + hi],
-                raw[:].rearrange("p j (m r) -> p m j r", r=PACK)[:, lo:hi],
+        def deal_w2(rounder, a, m0, m1):
+            rounder(
+                w2_bf[a][:].rearrange("p (i m j) -> p m j i", i=PACK, j=PACK)[:, m0:m1],
+                w2_raw[a][:].rearrange("p j (m i) -> p m j i", i=PACK)[:, m0:m1],
             )
 
-        def deal_w1(a, raw):
+        def deal_w1(a):
             nc.vector.tensor_copy(
-                out=w1_codes[a][:].bitcast(I32).rearrange("p (r g e) -> p g r e", r=PACK, e=4),
-                in_=raw[:].rearrange("p (g e r) -> p g r e", r=PACK, e=4),
+                out=w1_codes[a][:].bitcast(I32).rearrange("p (i g e) -> p g i e", i=PACK, e=LINE),
+                in_=w1_raw[a][:].rearrange("p (g e i) -> p g i e", i=PACK, e=LINE),
             )
 
-        def deal_w0(a, raw):
+        def deal(dst, src):
             nc.vector.tensor_copy(
-                out=w0_codes[a][:].bitcast(U16).rearrange("p (h r m) -> p h r m", h=2, r=2),
-                in_=raw[:].bitcast(U16).rearrange("p (m h r) -> p h r m", h=2, r=2),
+                out=dst.rearrange("p (a i m) -> p a i m", i=PACK, m=P),
+                in_=src.rearrange("p (a m i) -> p a i m", i=PACK, m=P),
             )
 
-        def deal_columns(dst, src):
-            nc.vector.tensor_copy(
-                out=dst.rearrange("p (a r m) -> p a r m", a=2, r=PACK),
-                in_=src.rearrange("p (a m r) -> p a r m", a=2, r=PACK),
-            )
+        def deal_w0(a):
+            deal(w0_codes[a][:].bitcast(U16), w0_raw[a][:].bitcast(U16))
 
-        def deal_scales(dst, src, a):
-            cols = slice(a * HALF, (a + 1) * HALF)
-            nc.vector.tensor_copy(
-                out=dst[:, cols].rearrange("p (h r m) -> p h r m", h=2, r=2),
-                in_=src[:, cols].rearrange("p (m h r) -> p h r m", h=2, r=2),
-            )
+        def deal_w1_scales(a):
+            deal(w1_plane[:, a * HALF : (a + 1) * HALF], s1_raw[:, a * HALF : (a + 1) * HALF])
 
         def quantize(codes, scales, src):
             nc.vector.quantize_mx(out=codes.bitcast(FP8X4), scales=scales, in_=src)
 
-        def quantize_x(c0, c1, x_bf):
-            quantize(x_codes[:, c0:c1], x_scales[:, c0:c1], x_bf)
+        def round_x(n):
+            interleave(round_on_vector, x_bf[n], x_raw[n], 0, X_CUTS[n + 1] - X_CUTS[n])
 
-        def one_pass(acc, tap, a, r, t0, n0, n1, start, stop):
-            cols = slice(r * P, (r + 1) * P)
-            both = slice(a * HALF + r * P, a * HALF + (r + 1) * P)
+        def quantize_x(n, c0, c1):
+            first = X_CUTS[n]
+            quantize(x_codes[:, c0:c1], x_plane[:, c0:c1], x_bf[n][:, PACK * (c0 - first) : PACK * (c1 - first)])
+
+        def quantize_w2(a, i0, i1):
+            cols = slice(i0 * P, i1 * P)
+            quantize(w2_codes[a][:, cols], w2_plane[a][:, cols], w2_bf[a][:, PACK * i0 * P : PACK * i1 * P])
+
+        banks, pos = [], []
+
+        def open_step(s):
+            width = steps[s][2]
+            group = []
+            for b in range(PACK * width // BANK):
+                acc = psum.tile([P, BANK], F32, name="acc")
+                group.append(acc)
+            banks.append(group)
+            positive = ring.tile([P, PACK * width], F32, name="pos", align_bytes=64)
+            pos.append(positive)
+
+        def one_pass(acc, tap, a, i, t, count, start, stop):
+            cols = slice(i * P, (i + 1) * P)
+            cols_of_both = slice(a * HALF + i * P, a * HALF + (i + 1) * P)
             if tap == 0:
-                lhsT = w0_codes[a][:, 2 * cols.start : 2 * cols.stop].bitcast(FP4X4)
-                lhsT_scale = w0_plane[:, both]
+                lhsT = w0_codes[a][:, 2 * i * P : 2 * (i + 1) * P].bitcast(FP4X4)
+                lhsT_scale = w0_plane[:, cols_of_both]
             elif tap == 1:
                 lhsT = w1_codes[a][:, cols].bitcast(FP8X4)
-                lhsT_scale = w1_plane[4:, both]
+                lhsT_scale = w1_plane[W1_PLANE:, cols_of_both]
             else:
                 lhsT = w2_codes[a][:, cols].bitcast(FP8X4)
                 lhsT_scale = w2_plane[a][:, cols]
-            window = slice(t0 + tap * D + n0, t0 + tap * D + n1)
+            window = slice(t + tap * D, t + tap * D + count)
             nc.tensor.matmul_mx(
-                out=acc[:, n0:n1],
+                out=acc,
                 lhsT=lhsT,
                 lhsT_scale=lhsT_scale,
                 rhs=x_codes[:, window].bitcast(FP8X4),
-                rhs_scale=x_scales[:, window],
+                rhs_scale=x_plane[:, window],
                 start=start,
                 stop=stop,
             )
 
-        def new_banks():
-            banks = []
-            for r in range(PACK):
-                acc = psum.tile([P, 512], F32, name="acc")
-                banks.append(acc)
-            return banks
-
-        def multiply(u, banks, rows, taps):
-            a, t0, width, on_vector = UNITS[u]
-            for r in rows:
+        def multiply(s, rows, taps):
+            tile, c0, width = steps[s]
+            a, t0 = TILES[tile]
+            for i in rows:
+                b, first = divmod(i * width, BANK)
                 for tap in taps:
-                    step = 128 if tap == 0 and width < 512 else width
-                    for n0 in range(0, width, step):
-                        one_pass(banks[r], tap, a, r, t0, n0, n0 + step, tap == 0 and n0 == 0, tap == 2)
+                    count = FP4_NARROW if tap == 0 and width == NARROW else width
+                    for n0 in range(0, width, count):
+                        one_pass(
+                            banks[s][b][:, first + n0 : first + n0 + count],
+                            tap, a, i, t0 + c0 + n0, count,
+                            start=(tap == 0 and first + n0 == 0),
+                            stop=(tap == 2 and first + width == BANK),
+                        )
 
-        def relu_scalar(u, r):
-            width = UNITS[u][2]
-            nc.scalar.activation(
-                out=pos[u][:, r * width : (r + 1) * width], in_=banks[u][r][:, :width], func=ACT.Relu
-            )
+        def relu_on_scalar(s, b):
+            nc.scalar.activation(out=pos[s][:, b * BANK : (b + 1) * BANK], in_=banks[s][b][:], func=ACT.Relu)
 
-        def relu_vector(u, r):
-            width = UNITS[u][2]
+        def relu_on_vector(s, b):
             nc.vector.tensor_scalar(
-                out=pos[u][:, r * width : (r + 1) * width],
-                in0=banks[u][r][:, :width],
-                scalar1=0.0,
-                scalar2=None,
-                op0=ALU.max,
+                out=pos[s][:, b * BANK : (b + 1) * BANK], in0=banks[s][b][:], scalar1=0.0, scalar2=None, op0=ALU.max
             )
 
-        def square(u, r0, r1):
-            width = UNITS[u][2]
-            cols = slice(r0 * width, r1 * width)
-            nc.scalar.activation(out=res[u][:, cols], in_=pos[u][:, cols], func=ACT.Square)
-
-        def square_vector(u, r0, r1):
-            width = UNITS[u][2]
-            cols = slice(r0 * width, r1 * width)
-            nc.vector.tensor_tensor(out=res[u][:, cols], in0=pos[u][:, cols], in1=pos[u][:, cols], op=ALU.mult)
-
-        def store_result(u, res, i0, i1):
-            a, t0, width, on_vector = UNITS[u]
-            rows = out_0[a * HALF : (a + 1) * HALF, t0 : t0 + width].rearrange("(p i) t -> p i t", i=PACK)
-            nc.sync.dma_start(
-                out=rows[:, i0:i1, :],
-                in_=res[:, i0 * width : i1 * width].rearrange("p (i t) -> p i t", t=width),
+        def square(s, b0, b1):
+            tile, c0, width = steps[s]
+            per_bank = BANK // width
+            nc.scalar.activation(
+                out=res[tile][:, b0 * per_bank : b1 * per_bank, c0 : c0 + width],
+                in_=pos[s][:, b0 * BANK : b1 * BANK].rearrange("p (i t) -> p i t", t=width),
+                func=ACT.Square,
             )
 
-        def round_result(u, res):
-            a, t0, width, on_vector = UNITS[u]
-            res_bf = ring.tile([P, PACK * width], BF16, name="res_bf", align_bytes=64)
-            interleave("vector", res_bf, res[:].rearrange("p (i t) -> p i t", i=PACK), 0, width)
-            return res_bf
-
-        def quantize_result(u, res_bf):
-            a, t0, width, on_vector = UNITS[u]
+        def quantize_result(tile, c0, c1, res_bf):
+            a, t0 = TILES[tile]
             if t0 < EARLY:
-                scales = early_scales[:, a * EARLY + t0 : a * EARLY + t0 + width]
+                scales = early_plane[:, a * EARLY + t0 + c0 : a * EARLY + t0 + c1]
             else:
-                first = a * (T - EARLY) + t0 - EARLY
-                scales = late_scales[:, first : first + width]
-            quantize(out_words[a][:, t0 : t0 + width], scales, res_bf[:])
+                scales = late_plane[:, a * (T - EARLY) + c0 : a * (T - EARLY) + c1]
+            quantize(out_codes[a][:, t0 + c0 : t0 + c1], scales, res_bf[:])
 
-        def store_words(a, t0, t1):
+        def store_result(tile, i0, i1, c0, c1):
+            a, t0 = TILES[tile]
+            rows = out_0[a * HALF : (a + 1) * HALF, t0 + c0 : t0 + c1].rearrange("(p i) t -> p i t", i=PACK)
+            nc.sync.dma_start(out=rows[:, i0:i1, :], in_=res[tile][:, i0:i1, c0:c1])
+
+        def store_codes(tile, c0, c1):
+            a, t0 = TILES[tile]
             nc.sync.dma_start(
-                out=out_1[a].rearrange("p t i -> p (t i)").bitcast(I32)[:, t0:t1],
-                in_=out_words[a][:, t0:t1].bitcast(I32),
+                out=out_1[a].rearrange("p t i -> p (t i)").bitcast(I32)[:, t0 + c0 : t0 + c1],
+                in_=out_codes[a][:, t0 + c0 : t0 + c1].bitcast(I32),
             )
 
-        def store_scales(queues, plane, t0, t1):
-            for q in range(4):
-                queues[q].dma_start(
-                    out=out_2[:, 4 * q : 4 * q + 4, t0:t1].bitcast(I32).rearrange("a r t -> r a t"),
-                    in_=plane[32 * q : 32 * q + 4, :].bitcast(I32).rearrange("r (a t) -> r a t", a=2),
+        def store_scale_rows(plane, t0, t1):
+            for r in range(4):
+                nc.sync.dma_start(
+                    out=out_2[:, r:16:4, t0:t1].bitcast(I32).rearrange("a q t -> q a t"),
+                    in_=plane[:].bitcast(I32)[r:P:32, :].rearrange("q (a t) -> q a t", a=2),
                 )
 
-        def open_unit(u):
-            banks.append(new_banks())
-            tile = ring.tile([P, PACK * UNITS[u][2]], F32, name="pos", align_bytes=64)
-            pos.append(tile)
-            res.append(kept("res%d" % u, [P, PACK * UNITS[u][2]], F32))
-
         rows = range(PACK)
-        banks, pos, res = [], [], []
-        x_bf0 = kept("x_bf0", [P, PACK * 512], BF16)
-        x_bf1 = kept("x_bf1", [P, PACK * 256], BF16)
-        x_bf2 = kept("x_bf2", [P, PACK * 256], BF16)
-        x_bf3 = kept("x_bf3", [P, PACK * 256], BF16)
-        x_bf4 = kept("x_bf4", [P, PACK * 512], BF16)
-        deal_w0(0, w0_raw0)
-        interleave("vector", x_bf0, x_raw0, 0, 256)
-        interleave("scalar", x_bf0, x_raw0, 256, 512)
-        deal_columns(w0_plane[:], s0_raw[:])
-        quantize_x(0, 256, x_bf0[:, :1024])
-        deal_w2("scalar", 0, w2_raw00, 0, 0, 64)
-        quantize_x(256, 512, x_bf0[:, 1024:])
-        deal_w2("vector", 0, w2_raw01, 64, 0, 44)
-        deal_w2("scalar", 0, w2_raw01, 64, 44, 64)
-        deal_scales(w1_plane, s1_raw, 0)
-        open_unit(0)
-        open_unit(1)
-        multiply(0, banks[0], rows, (0,))
-        multiply(1, banks[1], rows, (0,))
-        for r in rows:
-            cols = slice(r * P, (r + 1) * P)
-            quantize(w2_codes[0][:, cols], w2_plane[0][:, cols], w2_bf[0][:, PACK * r * P : PACK * (r + 1) * P])
-            if r == 0:
-                deal_w1(0, w1_raw0)
-            multiply(0, banks[0], (r,), (1, 2))
-        interleave("scalar", x_bf1, x_raw1, 0, 96)
-        interleave("vector", x_bf1, x_raw1, 96, 256)
-        quantize_x(512, 768, x_bf1[:])
-        multiply(1, banks[1], rows, (1, 2))
+        deal_w0(0)
+        interleave(round_on_vector, x_bf[0], x_raw[0], 0, NARROW)
+        interleave(round_on_scalar, x_bf[0], x_raw[0], NARROW, 2 * NARROW)
+        deal(w0_plane[:], s0_raw[:])
+        quantize_x(0, 0, NARROW)
+        quantize_x(0, NARROW, 2 * NARROW)
+        deal_w2(round_on_vector, 0, 0, W2_ON_VECTOR)
+        deal_w2(round_on_scalar, 0, W2_ON_VECTOR, P)
+        deal_w1_scales(0)
+        for s in (0, 1):
+            open_step(s)
+            multiply(s, rows, (0,))
+        for i in rows:
+            quantize_w2(0, i, i + 1)
+            if i == 0:
+                deal_w1(0)
+            multiply(0, (i,), (1, 2))
+        round_x(1)
+        deal_w1_scales(1)
+        quantize_x(1, X_CUTS[1], X_CUTS[2])
+        multiply(1, rows, (1, 2))
 
-        last = len(UNITS) - 1
-        res_bf = None
-        for u in range(len(UNITS)):
-            a, t0, width, on_vector = UNITS[u]
-            on_scalar = [r for r in rows if r not in on_vector]
-            ahead = ()
-            if 0 < u < last:
-                open_unit(u + 1)
-                multiply(u + 1, banks[u + 1], rows, (0, 1, 2))
-                ahead = UNITS[u + 1][3]
-            if u == 0:
-                interleave("vector", x_bf2, x_raw2, 0, 256)
-            if u == 1:
-                interleave("vector", x_bf3, x_raw3, 0, 256)
-            if u == 2:
-                deal_w2("vector", 1, w2_raw1, 0, 0, 128)
-            if u == 3:
-                interleave("vector", x_bf4, x_raw4, 0, 512)
-            if u > 0:
-                res_bf = round_result(u - 1, res[u - 1])
-            for r in ahead[:AHEAD[u + 1]]:
-                relu_vector(u + 1, r)
-            if u == 0:
-                quantize_x(768, 1024, x_bf2[:])
-            if u == 1:
-                quantize_x(1024, 1280, x_bf3[:])
-            if u == 2:
-                quantize(w2_codes[1][:], w2_plane[1][:], w2_bf[1][:])
-            if u == 3:
-                quantize_x(1280, 1792, x_bf4[:])
-            if u > 0:
-                quantize_result(u - 1, res_bf)
-            if u == 1:
-                deal_w0(1, w0_raw1)
-                deal_w1(1, w1_raw1)
-                deal_scales(w1_plane, s1_raw, 1)
-            relu_scalar(u, on_scalar[0])
-            for n in range(len(on_scalar)):
-                if n + 1 < len(on_scalar):
-                    relu_scalar(u, on_scalar[n + 1])
-                square(u, on_scalar[n], on_scalar[n] + 1)
-            for r in ahead[AHEAD[u + 1]:]:
-                relu_vector(u + 1, r)
-            split = len(on_vector)
-            store_result(u, res[u], split, 4)
-            if u > 0:
-                before = UNITS[u - 1]
-                store_words(before[0], before[1], before[1] + before[2])
-            if split > 0:
-                square(u, 0, split)
-                store_result(u, res[u], 0, split)
-            if u == 6:
-                store_scales([nc.sync] * 4, early_scales, 0, EARLY)
-        res_bf = round_result(last, res[last])
-        quantize_result(last, res_bf)
-        store_words(1, UNITS[last][1], T)
-        store_scales([nc.sync, nc.scalar, nc.sync, nc.scalar], late_scales, EARLY, T)
+        for s in range(len(steps)):
+            tile, c0, width = steps[s]
+            on_vector = len(banks[s]) // 2 if s >= first_wide else 0
+            ahead = []
+            if 0 < s < last:
+                open_step(s + 1)
+                if s + 1 == first_wide:
+                    multiply(s + 1, rows, (0, 1))
+                    multiply(s + 1, rows, (2,))
+                else:
+                    multiply(s + 1, rows, (0, 1, 2))
+                if s + 1 >= first_wide:
+                    ahead = list(range(len(banks[s + 1]) // 2))
+
+            done = None
+            if s > 0 and s != first_wide - 1:
+                before, b0, before_width = steps[s - 1]
+                done = (before, 0 if s == first_wide else b0, b0 + before_width)
+
+            if s == 0:
+                round_x(2)
+                quantize_x(2, X_CUTS[2], X_CUTS[3])
+            if s == 1:
+                round_x(3)
+            if s == 2:
+                deal_w2(round_on_vector, 1, 0, P)
+            if s == 3:
+                round_x(4)
+            if done:
+                res_bf = ring.tile([P, PACK * (done[2] - done[1])], BF16, name="res_bf", align_bytes=64)
+                interleave(round_on_vector, res_bf, res[done[0]][:, :, done[1] : done[2]], 0, done[2] - done[1])
+            for b in ahead[:1]:
+                relu_on_vector(s + 1, b)
+            if s == 1:
+                quantize_x(3, X_CUTS[3], X_CUTS[4])
+                deal_w0(1)
+            if s == 2:
+                quantize_w2(1, 0, PACK)
+            if s == 3:
+                quantize_x(4, X_CUTS[4], X_CUTS[5])
+            if done:
+                quantize_result(*done, res_bf)
+            if s == 1:
+                deal_w1(1)
+            for b in ahead[1:]:
+                relu_on_vector(s + 1, b)
+
+            if width == BANK:
+                relu_on_scalar(s, 2)
+                relu_on_scalar(s, 3)
+                square(s, 2, 3)
+                square(s, 3, 4)
+                store_result(tile, 2, 4, 0, BANK)
+                square(s, 0, 2)
+                store_result(tile, 0, 2, 0, BANK)
+            else:
+                for b in range(on_vector, 2):
+                    relu_on_scalar(s, b)
+                square(s, 0, 1)
+                square(s, 1, 2)
+                if tile == len(TILES) - 1:
+                    store_result(tile, 0, PACK, c0, c0 + width)
+                elif c0 + width == BANK:
+                    store_result(tile, 0, PACK, 0, BANK)
+
+            if done and s == last:
+                store_codes(*done)
+            elif done and done[2] == BANK:
+                store_codes(done[0], 0, BANK)
+                if TILES[done[0]] == (1, EARLY - BANK):
+                    store_scale_rows(early_plane, 0, EARLY)
+
+        tile, c0, width = steps[last]
+        res_bf = ring.tile([P, PACK * width], BF16, name="res_bf", align_bytes=64)
+        interleave(round_on_scalar, res_bf, res[tile][:, :, c0:], 0, LAST_ON_SCALAR)
+        interleave(round_on_vector, res_bf, res[tile][:, :, c0:], LAST_ON_SCALAR, width)
+        quantize_result(tile, c0, BANK, res_bf)
+        store_codes(tile, c0, BANK)
+        store_scale_rows(late_plane, EARLY, T)

from contextlib import ExitStack

import concourse.mybir as mybir

D, K, M, T = 128, 512, 1024, 1536
FLOPS = 2 * 3 * K * M * T

F32 = mybir.dt.float32
BF16 = mybir.dt.bfloat16
I32 = mybir.dt.int32
U32 = mybir.dt.uint32
U16 = mybir.dt.uint16
U8 = mybir.dt.uint8
FP8X4 = mybir.dt.float8_e4m3fn_x4
FP4X4 = mybir.dt.float4_e2m1fn_x4
ACT = mybir.ActivationFunctionType
ALU = mybir.AluOpType

P = 128
PACK = 4
HALF = P * PACK
BANK = 512
NARROW = BANK // 2
FP4_NARROW = 128
LINE = 4
W1_PLANE = 4
EARLY = 2 * BANK

TILES = [(0, 0), (0, BANK), (1, 0), (1, BANK), (0, 2 * BANK), (1, 2 * BANK)]
NARROW_TILES = (0, 1, len(TILES) - 1)
X_CUTS = [0, 512, 768, 1024, 1280, T + 2 * D]
W2_ON_VECTOR = 84
LAST_ON_SCALAR = 72


def tile_mix_dconv_fm_pl_relu2_kernel(
    tc, x, w0_words, w0_scales, w1_words, w1_scales, w2, out_0, out_1, out_2
):
    nc = tc.nc
    steps = []
    for tile in range(len(TILES)):
        width = NARROW if tile in NARROW_TILES else BANK
        steps.extend((tile, c0, width) for c0 in range(0, BANK, width))
    last = len(steps) - 1
    first_wide = 4

    with ExitStack() as ctx:
        keep = ctx.enter_context(tc.tile_pool(name="keep", bufs=1))
        ring = ctx.enter_context(tc.tile_pool(name="ring", bufs=3))
        psum = ctx.enter_context(tc.psum_pool(name="psum", bufs=8))
        ctx.enter_context(tc.manual_schedule())

        def kept(name, shape, dtype):
            return keep.tile(shape, dtype, name=name, align_bytes=64)

        x_codes = kept("x_codes", [P, X_CUTS[-1]], U32)
        x_plane = kept("x_plane", [P, X_CUTS[-1]], U8)
        w0_codes = [kept("w0_codes%d" % a, [P, 2 * HALF], U8) for a in range(2)]
        w0_plane = kept("w0_plane", [P, M], U8)
        w1_codes = [kept("w1_codes%d" % a, [P, HALF], U32) for a in range(2)]
        w1_plane = kept("w1_plane", [P, M], U8)
        w2_codes = [kept("w2_codes%d" % a, [P, HALF], U32) for a in range(2)]
        w2_plane = [kept("w2_plane%d" % a, [P, HALF], U8) for a in range(2)]
        w2_bf = [kept("w2_bf%d" % a, [P, PACK * HALF], BF16) for a in range(2)]
        x_bf = [
            kept("x_bf%d" % n, [P, PACK * (X_CUTS[n + 1] - X_CUTS[n])], BF16) for n in range(len(X_CUTS) - 1)
        ]
        res = [kept("res%d" % tile, [P, PACK, BANK], F32) for tile in range(len(TILES))]
        out_codes = [kept("out_codes%d" % a, [P, T], U32) for a in range(2)]
        early_plane = kept("early_plane", [P, 2 * EARLY], U8)
        late_plane = kept("late_plane", [P, 2 * (T - EARLY)], U8)

        def load_rows(name, src, c0, c1):
            raw = kept(name, [P, PACK, c1 - c0], F32)
            nc.sync.dma_start(out=raw[:], in_=src[:, c0:c1].rearrange("(p j) c -> p j c", j=PACK))
            return raw

        def load_x(n):
            return load_rows("x_raw%d" % n, x, X_CUTS[n], X_CUTS[n + 1])

        def load_w0(a):
            raw = kept("w0_raw%d" % a, [P, 2 * HALF], U8)
            pairs = w0_words[0].bitcast(I32)
            nc.sync.dma_start(out=raw[:].bitcast(I32), in_=pairs[:, a * HALF // 2 : (a + 1) * HALF // 2])
            return raw

        def load_w1(a):
            raw = kept("w1_raw%d" % a, [P, HALF], I32)
            words = w1_words[0].rearrange("p n i -> p (n i)").bitcast(I32)
            nc.sync.dma_start(out=raw[:], in_=words[:, a * HALF : (a + 1) * HALF])
            return raw

        def load_scale_rows(raw, src, first):
            for r in range(4):
                nc.sync.dma_start(
                    out=raw[:].bitcast(I32)[first + r : P : 32, :], in_=src[0].bitcast(I32)[r:16:4, :]
                )

        s0_raw = kept("s0_raw", [P, M], U8)
        s1_raw = kept("s1_raw", [P, M], U8)
        nc.vector.memset(s0_raw[:].bitcast(I32), 0)
        nc.vector.memset(s1_raw[:].bitcast(I32), 0)

        w0_raw, w1_raw, w2_raw, x_raw = [], [], [], []
        w0_raw.append(load_w0(0))
        x_raw.append(load_x(0))
        load_scale_rows(s0_raw, w0_scales, 0)
        w2_raw.append(load_rows("w2_raw0", w2, 0, HALF))
        load_scale_rows(s1_raw, w1_scales, W1_PLANE)
        w1_raw.append(load_w1(0))
        x_raw.extend(load_x(n) for n in (1, 2, 3))
        w0_raw.append(load_w0(1))
        w1_raw.append(load_w1(1))
        w2_raw.append(load_rows("w2_raw1", w2, HALF, M))
        x_raw.append(load_x(4))

        def round_on_vector(dst, src):
            nc.vector.tensor_copy(out=dst, in_=src)

        def round_on_scalar(dst, src):
            nc.scalar.activation(out=dst, in_=src, func=ACT.Copy)

        def interleave(rounder, dst, src, c0, c1):
            rounder(
                dst[:, PACK * c0 : PACK * c1].rearrange("p (g e j) -> p g j e", e=LINE, j=PACK),
                src[:, :, c0:c1].rearrange("p j (g e) -> p g j e", e=LINE),
            )

        def deal_w2(rounder, a, m0, m1):
            rounder(
                w2_bf[a][:].rearrange("p (i m j) -> p m j i", i=PACK, j=PACK)[:, m0:m1],
                w2_raw[a][:].rearrange("p j (m i) -> p m j i", i=PACK)[:, m0:m1],
            )

        def deal_w1(a):
            nc.vector.tensor_copy(
                out=w1_codes[a][:].bitcast(I32).rearrange("p (i g e) -> p g i e", i=PACK, e=LINE),
                in_=w1_raw[a][:].rearrange("p (g e i) -> p g i e", i=PACK, e=LINE),
            )

        def deal(dst, src):
            nc.vector.tensor_copy(
                out=dst.rearrange("p (a i m) -> p a i m", i=PACK, m=P),
                in_=src.rearrange("p (a m i) -> p a i m", i=PACK, m=P),
            )

        def deal_w0(a):
            deal(w0_codes[a][:].bitcast(U16), w0_raw[a][:].bitcast(U16))

        def deal_w1_scales(a):
            deal(w1_plane[:, a * HALF : (a + 1) * HALF], s1_raw[:, a * HALF : (a + 1) * HALF])

        def quantize(codes, scales, src):
            nc.vector.quantize_mx(out=codes.bitcast(FP8X4), scales=scales, in_=src)

        def round_x(n):
            interleave(round_on_vector, x_bf[n], x_raw[n], 0, X_CUTS[n + 1] - X_CUTS[n])

        def quantize_x(n, c0, c1):
            first = X_CUTS[n]
            quantize(x_codes[:, c0:c1], x_plane[:, c0:c1], x_bf[n][:, PACK * (c0 - first) : PACK * (c1 - first)])

        def quantize_w2(a, i0, i1):
            cols = slice(i0 * P, i1 * P)
            quantize(w2_codes[a][:, cols], w2_plane[a][:, cols], w2_bf[a][:, PACK * i0 * P : PACK * i1 * P])

        banks, pos = [], []

        def open_step(s):
            width = steps[s][2]
            group = []
            for b in range(PACK * width // BANK):
                acc = psum.tile([P, BANK], F32, name="acc")
                group.append(acc)
            banks.append(group)
            positive = ring.tile([P, PACK * width], F32, name="pos", align_bytes=64)
            pos.append(positive)

        def one_pass(acc, tap, a, i, t, count, start, stop):
            cols = slice(i * P, (i + 1) * P)
            cols_of_both = slice(a * HALF + i * P, a * HALF + (i + 1) * P)
            if tap == 0:
                lhsT = w0_codes[a][:, 2 * i * P : 2 * (i + 1) * P].bitcast(FP4X4)
                lhsT_scale = w0_plane[:, cols_of_both]
            elif tap == 1:
                lhsT = w1_codes[a][:, cols].bitcast(FP8X4)
                lhsT_scale = w1_plane[W1_PLANE:, cols_of_both]
            else:
                lhsT = w2_codes[a][:, cols].bitcast(FP8X4)
                lhsT_scale = w2_plane[a][:, cols]
            window = slice(t + tap * D, t + tap * D + count)
            nc.tensor.matmul_mx(
                out=acc,
                lhsT=lhsT,
                lhsT_scale=lhsT_scale,
                rhs=x_codes[:, window].bitcast(FP8X4),
                rhs_scale=x_plane[:, window],
                start=start,
                stop=stop,
            )

        def multiply(s, rows, taps):
            tile, c0, width = steps[s]
            a, t0 = TILES[tile]
            for i in rows:
                b, first = divmod(i * width, BANK)
                for tap in taps:
                    count = FP4_NARROW if tap == 0 and width == NARROW else width
                    for n0 in range(0, width, count):
                        one_pass(
                            banks[s][b][:, first + n0 : first + n0 + count],
                            tap, a, i, t0 + c0 + n0, count,
                            start=(tap == 0 and first + n0 == 0),
                            stop=(tap == 2 and first + width == BANK),
                        )

        def relu_on_scalar(s, b):
            nc.scalar.activation(out=pos[s][:, b * BANK : (b + 1) * BANK], in_=banks[s][b][:], func=ACT.Relu)

        def relu_on_vector(s, b):
            nc.vector.tensor_scalar(
                out=pos[s][:, b * BANK : (b + 1) * BANK], in0=banks[s][b][:], scalar1=0.0, scalar2=None, op0=ALU.max
            )

        def square(s, b0, b1):
            tile, c0, width = steps[s]
            per_bank = BANK // width
            nc.scalar.activation(
                out=res[tile][:, b0 * per_bank : b1 * per_bank, c0 : c0 + width],
                in_=pos[s][:, b0 * BANK : b1 * BANK].rearrange("p (i t) -> p i t", t=width),
                func=ACT.Square,
            )

        def quantize_result(tile, c0, c1, res_bf):
            a, t0 = TILES[tile]
            if t0 < EARLY:
                scales = early_plane[:, a * EARLY + t0 + c0 : a * EARLY + t0 + c1]
            else:
                scales = late_plane[:, a * (T - EARLY) + c0 : a * (T - EARLY) + c1]
            quantize(out_codes[a][:, t0 + c0 : t0 + c1], scales, res_bf[:])

        def store_result(tile, i0, i1, c0, c1):
            a, t0 = TILES[tile]
            rows = out_0[a * HALF : (a + 1) * HALF, t0 + c0 : t0 + c1].rearrange("(p i) t -> p i t", i=PACK)
            nc.sync.dma_start(out=rows[:, i0:i1, :], in_=res[tile][:, i0:i1, c0:c1])

        def store_codes(tile, c0, c1):
            a, t0 = TILES[tile]
            nc.sync.dma_start(
                out=out_1[a].rearrange("p t i -> p (t i)").bitcast(I32)[:, t0 + c0 : t0 + c1],
                in_=out_codes[a][:, t0 + c0 : t0 + c1].bitcast(I32),
            )

        def store_scale_rows(plane, t0, t1):
            for r in range(4):
                nc.sync.dma_start(
                    out=out_2[:, r:16:4, t0:t1].bitcast(I32).rearrange("a q t -> q a t"),
                    in_=plane[:].bitcast(I32)[r:P:32, :].rearrange("q (a t) -> q a t", a=2),
                )

        rows = range(PACK)
        deal_w0(0)
        interleave(round_on_vector, x_bf[0], x_raw[0], 0, NARROW)
        interleave(round_on_scalar, x_bf[0], x_raw[0], NARROW, 2 * NARROW)
        deal(w0_plane[:], s0_raw[:])
        quantize_x(0, 0, NARROW)
        quantize_x(0, NARROW, 2 * NARROW)
        deal_w2(round_on_vector, 0, 0, W2_ON_VECTOR)
        deal_w2(round_on_scalar, 0, W2_ON_VECTOR, P)
        deal_w1_scales(0)
        for s in (0, 1):
            open_step(s)
            multiply(s, rows, (0,))
        for i in rows:
            quantize_w2(0, i, i + 1)
            if i == 0:
                deal_w1(0)
            multiply(0, (i,), (1, 2))
        round_x(1)
        deal_w1_scales(1)
        quantize_x(1, X_CUTS[1], X_CUTS[2])
        multiply(1, rows, (1, 2))

        for s in range(len(steps)):
            tile, c0, width = steps[s]
            on_vector = len(banks[s]) // 2 if s >= first_wide else 0
            ahead = []
            if 0 < s < last:
                open_step(s + 1)
                if s + 1 == first_wide:
                    multiply(s + 1, rows, (0, 1))
                    multiply(s + 1, rows, (2,))
                else:
                    multiply(s + 1, rows, (0, 1, 2))
                if s + 1 >= first_wide:
                    ahead = list(range(len(banks[s + 1]) // 2))

            done = None
            if s > 0 and s != first_wide - 1:
                before, b0, before_width = steps[s - 1]
                done = (before, 0 if s == first_wide else b0, b0 + before_width)

            if s == 0:
                round_x(2)
                quantize_x(2, X_CUTS[2], X_CUTS[3])
            if s == 1:
                round_x(3)
            if s == 2:
                deal_w2(round_on_vector, 1, 0, P)
            if s == 3:
                round_x(4)
            if done:
                res_bf = ring.tile([P, PACK * (done[2] - done[1])], BF16, name="res_bf", align_bytes=64)
                interleave(round_on_vector, res_bf, res[done[0]][:, :, done[1] : done[2]], 0, done[2] - done[1])
            for b in ahead[:1]:
                relu_on_vector(s + 1, b)
            if s == 1:
                quantize_x(3, X_CUTS[3], X_CUTS[4])
                deal_w0(1)
            if s == 2:
                quantize_w2(1, 0, PACK)
            if s == 3:
                quantize_x(4, X_CUTS[4], X_CUTS[5])
            if done:
                quantize_result(*done, res_bf)
            if s == 1:
                deal_w1(1)
            for b in ahead[1:]:
                relu_on_vector(s + 1, b)

            if width == BANK:
                relu_on_scalar(s, 2)
                relu_on_scalar(s, 3)
                square(s, 2, 3)
                square(s, 3, 4)
                store_result(tile, 2, 4, 0, BANK)
                square(s, 0, 2)
                store_result(tile, 0, 2, 0, BANK)
            else:
                for b in range(on_vector, 2):
                    relu_on_scalar(s, b)
                square(s, 0, 1)
                square(s, 1, 2)
                if tile == len(TILES) - 1:
                    store_result(tile, 0, PACK, c0, c0 + width)
                elif c0 + width == BANK:
                    store_result(tile, 0, PACK, 0, BANK)

            if done and s == last:
                store_codes(*done)
            elif done and done[2] == BANK:
                store_codes(done[0], 0, BANK)
                if TILES[done[0]] == (1, EARLY - BANK):
                    store_scale_rows(early_plane, 0, EARLY)

        tile, c0, width = steps[last]
        res_bf = ring.tile([P, PACK * width], BF16, name="res_bf", align_bytes=64)
        interleave(round_on_scalar, res_bf, res[tile][:, :, c0:], 0, LAST_ON_SCALAR)
        interleave(round_on_vector, res_bf, res[tile][:, :, c0:], LAST_ON_SCALAR, width)
        quantize_result(tile, c0, BANK, res_bf)
        store_codes(tile, c0, BANK)
        store_scale_rows(late_plane, EARLY, T)
